import numpy as np
import ml_dtypes


def mxq(x, axis, fmt="e4m3"):
    dtype, down = {"e4m3": (ml_dtypes.float8_e4m3fn, 7), "e5m2": (ml_dtypes.float8_e5m2, 14)}[fmt]
    v = np.moveaxis(np.asarray(x, np.float32).astype(ml_dtypes.bfloat16).astype(np.float64), axis, -1)
    blocks = v.reshape(v.shape[:-1] + (-1, 32))
    amax = np.abs(blocks).max(-1, keepdims=True)
    byte = np.maximum(np.where(amax > 0, np.frexp(amax)[1] - 1 + 127, 0) - down, 1)
    scale = np.exp2(byte - 127.0)
    codes = (blocks / scale).astype(np.float32).astype(dtype).astype(np.float64)
    return np.moveaxis((codes * scale).reshape(v.shape), -1, axis)


WIDE = False


def mx_kscale(k):
    if not WIDE:
        return np.ones(k)
    levels = np.array([10, -10, 5, -5, 0])
    if k % 512:
        return np.exp2(np.random.permutation(np.resize(levels, k // 32))).repeat(32)
    a = np.empty((k // 512, 16))
    for p in range(k // 512):
        a[p, :8] = np.random.permutation(np.resize(levels, 8))
        for g in range(8):
            far = levels[np.abs(levels - a[p, g]) >= 10]
            a[p, g + 8] = far[np.random.randint(len(far))]
    return np.exp2(a.ravel()).repeat(32)


def f64(x):
    return np.asarray(x).astype(np.float64)


def striped(idx):
    return np.tile(idx.reshape(-1, 16).T, (8, 1)).astype(np.uint16)


def unstriped(offs):
    return offs[:16].T.reshape(-1).astype(np.int64)


E2M1 = np.array([0.0, 0.5, 1.0, 1.5, 2.0, 3.0, 4.0, 6.0, -0.0, -0.5, -1.0, -1.5, -2.0, -3.0, -4.0, -6.0])


def pack_weight(w, fmt):
    k, n = w.shape
    w = f64(np.asarray(w, np.float32).astype(ml_dtypes.bfloat16)).reshape(k // 32, 32, n)
    amax = np.abs(w).max(1)
    if fmt == "e4m3":
        byte = np.frexp(amax)[1] - 1 + 127 - 7
    else:
        mant, ex = np.frexp(amax / 6.0)
        byte = np.where(mant > 0.5, ex, ex - 1) + 127
    byte = np.clip(np.where(amax > 0, byte, 1), 1, 254)
    scaled = (w * np.exp2(127.0 - byte)[:, None, :]).reshape(k, n).astype(np.float32)
    by_word = np.ascontiguousarray(scaled.reshape(k // 512, 128, 4, n).transpose(0, 1, 3, 2))
    if fmt == "e4m3":
        words = by_word.astype(ml_dtypes.float8_e4m3fn).view(np.uint8)
    else:
        c = by_word.astype(ml_dtypes.float4_e2m1fn).view(np.uint8) & 0xF
        words = (c[..., 0::2] | (c[..., 1::2] << 4)).reshape(k // 512, 128, 2 * n)
    return np.ascontiguousarray(words), np.ascontiguousarray(byte.astype(np.uint8).reshape(k // 512, 16, n))


def unpack_weight(words, scales, fmt):
    g, _, n = scales.shape
    words = np.ascontiguousarray(words).reshape(g, 128, n, -1)
    if fmt == "e4m3":
        vals = words.view(ml_dtypes.float8_e4m3fn).astype(np.float64)
    else:
        nib = np.empty((g, 128, n, 4), np.uint8)
        nib[..., 0::2] = words & 0xF
        nib[..., 1::2] = words >> 4
        vals = E2M1[nib]
    vals = vals * np.repeat(np.exp2(scales.astype(np.float64) - 127.0), 8, axis=1)[..., None]
    return vals.transpose(0, 1, 3, 2).reshape(g * 512, n)


def gelu(v):
    return 0.5 * v * (1.0 + np.tanh(np.sqrt(2.0 / np.pi) * (v + 0.044715 * v**3)))


K, K2, H, N, T, S, P, T2 = 1024, 512, 1024, 512, 2048, 1024, 512, 2048

def setup_inputs():
    n = np.random.standard_normal
    s, s2, u = mx_kscale(K)[:, None], mx_kscale(K2)[:, None], mx_kscale(H)[:, None]
    tab_words, tab_scales = pack_weight(n((K, T)) * s, "e4m3")
    tab2_words, tab2_scales = pack_weight(n((K2, T)) * s2, "e4m3")
    w3_words, w3_scales = pack_weight(1.3 * n((H, N)) / np.sqrt(H) / u, "e2m1")
    w5_words, w5_scales = pack_weight(n((K, N)) / np.sqrt(K) / s, "e4m3")
    perm = np.random.permutation(T2)
    return {
        "tab_words": tab_words, "tab_scales": tab_scales,
        "tab2_words": tab2_words, "tab2_scales": tab2_scales,
        "offs": striped(np.random.permutation(T)[:S]),
        "offs2": striped(np.random.permutation(T)[:P]),
        "pos1": striped(np.random.permutation(S)[:P]),
        "offs3": striped(perm[:S]), "offs4": striped(perm[S:S + P]),
        "w1": (1.3 * n((K, H)) / np.sqrt(K) / s).astype(np.float32),
        "w2": (n((K2, H)) / np.sqrt(K2) / s2 * u.T).astype(np.float32),
        "w3_words": w3_words, "w3_scales": w3_scales,
        "w4": (n((H, N)) / np.sqrt(H) / u).astype(np.float32),
        "w5_words": w5_words, "w5_scales": w5_scales,
        "gain": (np.exp(0.3 * n(H)) * u[:, 0]).astype(np.float32),
        "page1": n((N, T2)).astype(np.float32),
        "wg1": np.exp(0.3 * n((128, S))).astype(np.float32),
        "wg2": np.exp(0.3 * n((128, P))).astype(np.float32)}

def reference(tab_words, tab_scales, tab2_words, tab2_scales, offs, offs2, pos1, offs3, offs4, w1, w2, w3_words, w3_scales, w4, w5_words, w5_scales, gain, page1, wg1, wg2):
    v = unpack_weight(tab_words, tab_scales, "e4m3")[:, unstriped(offs)]
    v2 = unpack_weight(tab2_words, tab2_scales, "e4m3")[:, unstriped(offs2)]
    h1 = mxq(f64(w1), 0, "e4m3").T @ v
    h2 = mxq(f64(w2), 0, "e4m3").T @ v2
    z1 = f64(gain)[:, None] * np.tanh(h1)
    z2 = h2 * h1[:, unstriped(pos1)]
    turn = unpack_weight(w5_words, w5_scales, "e4m3").T @ v
    y1 = (unpack_weight(w3_words, w3_scales, "e2m1").T @ mxq(z1, 0, "e4m3")) * turn
    y2 = mxq(f64(w4), 0, "e4m3").T @ mxq(z2, 0, "e4m3")
    out = f64(page1).copy()
    out[:, unstriped(offs3)] = np.tile(f64(wg1), (N // 128, 1)) * y1
    out[:, unstriped(offs4)] = np.tile(f64(wg2), (N // 128, 1)) * y2
    return out

@@ -1,0 +1,339 @@
+from contextlib import ExitStack
+
+import concourse.mybir as mybir
+
+K, K2, H, N, T, S, P2, T2 = 1024, 512, 1024, 512, 2048, 1024, 512, 2048
+FLOPS = 2 * (K * H * S + K2 * H * P2 + K * N * S + H * N * S + H * N * P2)
+
+F32 = mybir.dt.float32
+BF16 = mybir.dt.bfloat16
+I32 = mybir.dt.int32
+U32 = mybir.dt.uint32
+U16 = mybir.dt.uint16
+U8 = mybir.dt.uint8
+FP8X4 = mybir.dt.float8_e4m3fn_x4
+FP4X4 = mybir.dt.float4_e2m1fn_x4
+MULT = mybir.AluOpType.mult
+COPY = mybir.ActivationFunctionType.Copy
+TANH = mybir.ActivationFunctionType.Tanh
+
+P = 128
+PASS = 512
+CHUNK = 256
+
+
+def tile_list_replenishment_slot_features_kernel(
+    tc, tab_words, tab_scales, tab2_words, tab2_scales, offs, offs2, pos1, offs3, offs4,
+    w1, w2, w3_words, w3_scales, w4, w5_words, w5_scales, gain, page1, wg1, wg2, out,
+):
+    nc = tc.nc
+    with ExitStack() as ctx:
+        keep = ctx.enter_context(tc.tile_pool(name="keep", bufs=1))
+        ring = ctx.enter_context(tc.tile_pool(name="ring", bufs=2))
+        psum = ctx.enter_context(tc.psum_pool(name="psum", bufs=1))
+
+        def held(shape, dtype, name):
+            return keep.tile(shape, dtype, name=name, align_bytes=64)
+
+        def load_list(src, name):
+            tile = keep.tile(list(src.shape), U16, name=name)
+            nc.sync.dma_start(tile[:], src)
+            return tile
+
+        def load_words(src, name):
+            tile = held([P, src.shape[1]], U32, name)
+            nc.sync.dma_start(tile[:].bitcast(I32), src.rearrange("p t i -> p (t i)").bitcast(I32))
+            return tile
+
+        def load_stacked_scales(queue, src, tile):
+            passes = src.shape[0]
+            for q in range(4):
+                queue.dma_start(
+                    tile[32 * q : 32 * q + 4 * passes, :].bitcast(I32),
+                    src[:, 4 * q : 4 * q + 4, :].bitcast(I32),
+                )
+
+        def zeroed(width, name):
+            tile = held([P, width], U8, name)
+            nc.vector.memset(tile[:].bitcast(I32), 0)
+            return tile
+
+        def load_rows(rows, name):
+            raw = ring.tile([P, 4, PASS], F32, name=name, tag="raw", bufs=5)
+            nc.sync.dma_start(raw[:], rows.rearrange("(p j) c -> p j c", j=4))
+            return raw
+
+        def copy_on(engine, dst, src):
+            if engine == "vector":
+                nc.vector.tensor_copy(dst, src)
+            else:
+                nc.scalar.copy(dst, src)
+
+        def interleave(engine, raw, deal_columns, name):
+            grouped = ring.tile([P, 4 * PASS], BF16, name=name, tag="grouped", bufs=3, align_bytes=64)
+            if deal_columns:
+                copy_on(
+                    engine,
+                    grouped[:].rearrange("p (t m j) -> p m j t", t=4, j=4),
+                    raw[:].rearrange("p j (m t) -> p m j t", t=4),
+                )
+            else:
+                copy_on(
+                    engine,
+                    grouped[:].rearrange("p (c i j) -> p c j i", i=4, j=4),
+                    raw[:].rearrange("p j (c i) -> p c j i", i=4),
+                )
+            return grouped
+
+        def quantize(grouped, codes, scales):
+            nc.vector.quantize_mx(out=codes[:].bitcast(FP8X4), scales=scales[:], in_=grouped[:])
+            return codes, scales
+
+        def quantize_held(grouped, name):
+            return quantize(grouped, held([P, PASS], U32, name + "_codes"), held([P, PASS], U8, name + "_scales"))
+
+        def gather(window, offsets, dtype, name):
+            picked = held([P, 16 * offsets.shape[1]], dtype, name)
+            nc.vector.tensor_copy(picked[:], window[:].indirect(offsets[:]))
+            return picked
+
+        offs_sb = load_list(offs, "offs_sb")
+        tab_scales_sb = zeroed(T, "tab_scales_sb")
+        w5_scales_sb = zeroed(N, "w5_scales_sb")
+        w3_scales_flat = zeroed(2 * N, "w3_scales_sb")
+        w3_scales_sb = w3_scales_flat[:].rearrange("p (a c) -> p a c", a=2)
+        tab2_scales_sb = zeroed(T, "tab2_scales_sb")
+        tab_sb = [None, None]
+        w1_raw = {}
+        gain_sb = held([P, 2, 4], F32, "gain_sb")
+        w5_sb = held([P, 2, N], U32, "w5_sb")
+        wg1_sb = held([P, S], F32, "wg1_sb")
+        w3_sb = held([P, 2, 2 * N], U8, "w3_sb")
+        wg2_sb = held([P, P2], F32, "wg2_sb")
+        pages = [held([P, T2], F32, "page%d" % nt) for nt in range(N // P)]
+
+        def load_page(nt):
+            nc.sync.dma_start(pages[nt][:], page1[nt * P : (nt + 1) * P, :])
+
+        load_stacked_scales(nc.gpsimd, w5_scales, w5_scales_sb)
+        for q in range(4):
+            nc.gpsimd.dma_start(
+                w3_scales_sb[32 * q : 32 * q + 4, :, :].bitcast(I32),
+                w3_scales[:, 4 * q : 4 * q + 4, :].rearrange("a r c -> r a c").bitcast(I32),
+            )
+        tab_sb[0] = load_words(tab_words[0], "tab_sb0")
+        load_stacked_scales(nc.sync, tab_scales, tab_scales_sb)
+        w1_raw[0, 0] = load_rows(w1[0:PASS, 0:PASS], "w1_raw00")
+        w1_raw[1, 0] = load_rows(w1[PASS : 2 * PASS, 0:PASS], "w1_raw10")
+        tab_sb[1] = load_words(tab_words[1], "tab_sb1")
+        w1_raw[0, 1] = load_rows(w1[0:PASS, PASS : 2 * PASS], "w1_raw01")
+        w1_raw[1, 1] = load_rows(w1[PASS : 2 * PASS, PASS : 2 * PASS], "w1_raw11")
+        nc.sync.dma_start(gain_sb[:], gain.rearrange("(b p t) -> p b t", b=2, t=4))
+        nc.sync.dma_start(w5_sb[:].bitcast(I32), w5_words.rearrange("a p c i -> p a (c i)").bitcast(I32))
+        nc.sync.dma_start(wg1_sb[:], wg1)
+        nc.sync.dma_start(w3_sb[:].bitcast(I32), w3_words.rearrange("a p c -> p a c").bitcast(I32))
+        offs3_sb = load_list(offs3, "offs3_sb")
+        load_page(0)
+        load_page(1)
+        offs2_sb = load_list(offs2, "offs2_sb")
+        tab2_sb = load_words(tab2_words[0], "tab2_sb")
+        load_stacked_scales(nc.sync, tab2_scales, tab2_scales_sb)
+        load_page(2)
+        load_page(3)
+        w2_raw = [load_rows(w2[:, 0:PASS], "w2_raw0")]
+        w2_raw.append(load_rows(w2[:, PASS : 2 * PASS], "w2_raw1"))
+        pos1_sb = load_list(pos1, "pos1_sb")
+        w4_raw = [load_rows(w4[a * PASS : (a + 1) * PASS, :], "w4_raw%d" % a) for a in range(2)]
+        nc.sync.dma_start(wg2_sb[:], wg2)
+        offs4_sb = load_list(offs4, "offs4_sb")
+
+        v_codes = [None, None]
+        w1_q = {}
+        v_codes[0] = gather(tab_sb[0], offs_sb, U32, "v_codes0")
+        v_scales = gather(tab_scales_sb, offs_sb, U8, "v_scales")
+        w1_q[0, 0] = quantize_held(interleave("scalar", w1_raw[0, 0], True, "w1_g00"), "w1_00")
+        v_codes[1] = gather(tab_sb[1], offs_sb, U32, "v_codes1")
+        w1_q[1, 0] = quantize_held(interleave("scalar", w1_raw[1, 0], True, "w1_g10"), "w1_10")
+        w1_q[0, 1] = quantize_held(interleave("vector", w1_raw[0, 1], True, "w1_g01"), "w1_01")
+        w1_q[1, 1] = quantize_held(interleave("vector", w1_raw[1, 1], True, "w1_g11"), "w1_11")
+
+        h1 = [[held([P, S], F32, "h1_%d%d" % (b, t)) for t in range(4)] for b in range(2)]
+
+        def times_v(acc, codes_of, scales_of, cols):
+            for a in range(2):
+                nc.tensor.matmul_mx(
+                    out=acc,
+                    lhsT=codes_of(a).bitcast(FP8X4),
+                    lhsT_scale=scales_of(a),
+                    rhs=v_codes[a][:, cols].bitcast(FP8X4),
+                    rhs_scale=v_scales[4 * a :, cols],
+                    start=(a == 0),
+                    stop=(a == 1),
+                )
+
+        h_banks = [psum.tile([P, 2, CHUNK], F32, name="h_bank%d" % i) for i in range(4)]
+        turn_banks = [psum.tile([P, 2, CHUNK], F32, name="turn_bank%d" % i) for i in range(2)]
+        y_banks = [psum.tile([P, 2, CHUNK], F32, name="y_bank%d" % i) for i in range(2)]
+
+        def make_z1(c, b, work, z1_bf, gain_engine):
+            cols = slice(c * CHUNK, (c + 1) * CHUNK)
+            for u in range(2):
+                bank = h_banks[2 * b + u]
+                for e in range(2):
+                    m_cols = slice((2 * u + e) * P, (2 * u + e + 1) * P)
+                    times_v(bank[:, e, :], lambda a: w1_q[a, b][0][:, m_cols], lambda a: w1_q[a, b][1][:, m_cols], cols)
+                half = work[:, u * 2 * CHUNK : (u + 1) * 2 * CHUNK]
+                if gain_engine == "vector":
+                    nc.scalar.activation(half.rearrange("p (n e) -> p n e", e=2), bank[:].rearrange("p e n -> p n e"), TANH)
+                else:
+                    nc.scalar.activation(half.rearrange("p (e n) -> p e n", e=2), bank[:], TANH)
+                for e in range(2):
+                    nc.scalar.copy(h1[b][2 * u + e][:, cols], bank[:, e, :])
+            if gain_engine == "vector":
+                nc.vector.tensor_tensor(
+                    z1_bf.rearrange("p (n u e) -> p n u e", u=2, e=2),
+                    work[:].rearrange("p (u n e) -> p n u e", u=2, e=2),
+                    gain_sb[:, b, :].rearrange("p (u e) -> p u e", u=2).unsqueeze(1).to_broadcast([P, CHUNK, 2, 2]),
+                    MULT,
+                )
+            else:
+                planes = ring.tile([P, 4, CHUNK], BF16, name="planes", bufs=2)
+                for t in range(4):
+                    nc.scalar.activation(
+                        planes[:, t, :], work[:, t * CHUNK : (t + 1) * CHUNK], COPY, scale=gain_sb[:, b, t : t + 1]
+                    )
+                nc.scalar.copy(
+                    z1_bf.rearrange("p (c i j) -> p c j i", i=4, j=4), planes[:].rearrange("p j (c i) -> p c j i", i=4)
+                )
+            codes = ring.tile([P, CHUNK], U32, name="z1_codes", bufs=4, align_bytes=64)
+            scales = ring.tile([P, CHUNK], U8, name="z1_scales", bufs=4, align_bytes=64)
+            nc.vector.quantize_mx(out=codes[:].bitcast(FP8X4), scales=scales[:], in_=z1_bf)
+            return codes, scales
+
+        def make_factor(c, pair, factor):
+            cols = slice(c * CHUNK, (c + 1) * CHUNK)
+            bank = turn_banks[pair]
+            for i in range(2):
+                m_cols = slice((2 * pair + i) * P, (2 * pair + i + 1) * P)
+                times_v(bank[:, i, :], lambda a: w5_sb[:, a, m_cols], lambda a: w5_scales_sb[4 * a :, m_cols], cols)
+            nc.vector.tensor_tensor(
+                factor.rearrange("p (i n) -> p i n", i=2),
+                bank[:],
+                wg1_sb[:, cols].unsqueeze(1).to_broadcast([P, 2, CHUNK]),
+                MULT,
+            )
+            return factor
+
+        def make_y1(z1_q, y1_sb):
+            for pair in range(2):
+                bank = y_banks[pair]
+                for i in range(2):
+                    nt = 2 * pair + i
+                    for a in range(2):
+                        nc.tensor.matmul_mx(
+                            out=bank[:, i, :],
+                            lhsT=w3_sb[:, a, 2 * nt * P : 2 * (nt + 1) * P].bitcast(FP4X4),
+                            lhsT_scale=w3_scales_sb[:, a, nt * P : (nt + 1) * P],
+                            rhs=z1_q[a][0][:].bitcast(FP8X4),
+                            rhs_scale=z1_q[a][1][:],
+                            start=(a == 0),
+                            stop=(a == 1),
+                        )
+                nc.scalar.copy(
+                    y1_sb[:, pair * 2 * CHUNK : (pair + 1) * 2 * CHUNK].rearrange("p (i n) -> p i n", i=2), bank[:]
+                )
+            return y1_sb
+
+        def put_y1(c, pair, y1_sb, factor):
+            places = offs3_sb[:, c * CHUNK // 16 : (c + 1) * CHUNK // 16]
+            for i in range(2):
+                nt = 2 * pair + i
+                nc.vector.tensor_tensor(
+                    pages[nt][:].indirect(places),
+                    y1_sb[:, nt * CHUNK : (nt + 1) * CHUNK],
+                    factor[:, i * CHUNK : (i + 1) * CHUNK],
+                    MULT,
+                )
+
+        def make_h2(w2_q, v2_codes, v2_scales):
+            h2_sb = ring.tile([P, 4, PASS], F32, name="h2_sb", tag="raw", bufs=5)
+            for t in range(4):
+                m_cols = slice(t * P, (t + 1) * P)
+                bank = h_banks[t][:].rearrange("p e n -> p (e n)")
+                nc.tensor.matmul_mx(
+                    out=bank,
+                    lhsT=w2_q[0][:, m_cols].bitcast(FP8X4),
+                    lhsT_scale=w2_q[1][:, m_cols],
+                    rhs=v2_codes[:].bitcast(FP8X4),
+                    rhs_scale=v2_scales[:],
+                    start=True,
+                    stop=True,
+                )
+                nc.scalar.copy(h2_sb[:, t, :], bank)
+            return h2_sb
+
+        def join(h2_sb, b):
+            z2_f = ring.tile([P, 4, PASS], F32, name="z2_f", tag="raw", bufs=5)
+            for t in range(4):
+                nc.vector.tensor_tensor(z2_f[:, t, :], h1[b][t][:].indirect(pos1_sb[:]), h2_sb[:, t, :], MULT)
+            return interleave("scalar", z2_f, False, "z2_g")
+
+        work = [held([P, 4 * CHUNK], F32, "work%d" % i) for i in range(4)]
+        gate = [held([P, 2 * CHUNK], F32, "gate%d" % i) for i in range(2)]
+
+        def fresh_bf():
+            tile = ring.tile([P, 4 * CHUNK], BF16, name="z1_bf", bufs=2, align_bytes=64)
+            return tile[:]
+
+        def fresh_factor():
+            tile = ring.tile([P, 2 * CHUNK], F32, name="factor", bufs=2)
+            return tile[:]
+
+        z00 = make_z1(0, 0, work[0], fresh_bf(), "vector")
+        z01 = make_z1(0, 1, work[2], gate[0][:].bitcast(BF16), "vector")
+        f00 = make_factor(0, 0, fresh_factor())
+        y0 = make_y1([z00, z01], work[3])
+        put_y1(0, 0, y0, f00)
+        z10 = make_z1(1, 0, work[1], fresh_bf(), "vector")
+        z11 = make_z1(1, 1, work[0], gate[1][:].bitcast(BF16), "vector")
+        put_y1(0, 1, y0, make_factor(0, 1, gate[1][:]))
+        f10 = make_factor(1, 0, fresh_factor())
+        z20 = make_z1(2, 0, work[1], fresh_bf(), "scalar")
+        y1 = make_y1([z10, z11], work[1])
+        put_y1(1, 0, y1, f10)
+        v2_codes = gather(tab2_sb, offs2_sb, U32, "v2_codes")
+        v2_scales = gather(tab2_scales_sb, offs2_sb, U8, "v2_scales")
+        z21 = make_z1(2, 1, work[2], gate[0][:].bitcast(BF16), "scalar")
+        put_y1(1, 1, y1, make_factor(1, 1, gate[0][:]))
+        f20 = make_factor(2, 0, fresh_factor())
+        w2_g = [interleave("scalar", w2_raw[b], True, "w2_g") for b in range(2)]
+        w2_q = [quantize_held(w2_g[b], "w2_%d" % b) for b in range(2)]
+        z30 = make_z1(3, 0, work[0], fresh_bf(), "scalar")
+        y2 = make_y1([z20, z21], work[0])
+        put_y1(2, 0, y2, f20)
+        z31 = make_z1(3, 1, work[2], gate[1][:].bitcast(BF16), "vector")
+        put_y1(2, 1, y2, make_factor(2, 1, gate[1][:]))
+        h2_sb = [make_h2(w2_q[b], v2_codes, v2_scales) for b in range(2)]
+        y3 = make_y1([z30, z31], work[3])
+        w4_q = [quantize_held(interleave("scalar", w4_raw[a], False, "w4_g"), "w4_%d" % a) for a in range(2)]
+        z2_g = [join(h2_sb[b], b) for b in range(2)]
+        put_y1(3, 0, y3, make_factor(3, 0, h2_sb[1][:, 3, :]))
+        z2_q = [quantize_held(z2_g[b], "z2_%d" % b) for b in range(2)]
+        put_y1(3, 1, y3, make_factor(3, 1, z2_g[1][:, 0 : 4 * CHUNK].bitcast(F32)))
+        for nt in range(N // P):
+            m_cols = slice(nt * P, (nt + 1) * P)
+            bank = h_banks[nt][:].rearrange("p e n -> p (e n)")
+            for a in range(2):
+                nc.tensor.matmul_mx(
+                    out=bank,
+                    lhsT=w4_q[a][0][:, m_cols].bitcast(FP8X4),
+                    lhsT_scale=w4_q[a][1][:, m_cols],
+                    rhs=z2_q[a][0][:].bitcast(FP8X4),
+                    rhs_scale=z2_q[a][1][:],
+                    start=(a == 0),
+                    stop=(a == 1),
+                )
+            y2_sb = ring.tile([P, P2], F32, name="y2_sb", bufs=2)
+            nc.scalar.copy(y2_sb[:], bank)
+            nc.vector.tensor_tensor(pages[nt][:].indirect(offs4_sb[:]), y2_sb[:], wg2_sb[:], MULT)
+            nc.sync.dma_start(out[m_cols, :], pages[nt][:])

@@ -41,7 +41,7 @@ def tile_list_replenishment_slot_features_kernel(
             return tile
 
         def load_words(src, name):
-            tile = held([P, src.shape[1]], U32, name)
+            tile = ring.tile([P, src.shape[1]], U32, name=name, tag="wide", bufs=3, align_bytes=64)
             nc.sync.dma_start(tile[:].bitcast(I32), src.rearrange("p t i -> p (t i)").bitcast(I32))
             return tile
 
@@ -58,8 +58,9 @@ def tile_list_replenishment_slot_features_kernel(
             nc.vector.memset(tile[:].bitcast(I32), 0)
             return tile
 
-        def load_rows(rows, name):
-            raw = ring.tile([P, 4, PASS], F32, name=name, tag="raw", bufs=5)
+        stage = [held([P, 4, PASS], F32, "stage%d" % i) for i in range(4)]
+
+        def load_rows(rows, raw):
             nc.sync.dma_start(raw[:], rows.rearrange("(p j) c -> p j c", j=4))
             return raw
 
@@ -69,8 +70,9 @@ def tile_list_replenishment_slot_features_kernel(
             else:
                 nc.scalar.copy(dst, src)
 
-        def interleave(engine, raw, deal_columns, name):
-            grouped = ring.tile([P, 4 * PASS], BF16, name=name, tag="grouped", bufs=3, align_bytes=64)
+        def interleave(engine, raw, deal_columns, name, grouped=None):
+            if grouped is None:
+                grouped = ring.tile([P, 4 * PASS], BF16, name=name, tag="grouped", bufs=3, align_bytes=64)
             if deal_columns:
                 copy_on(
                     engine,
@@ -123,29 +125,11 @@ def tile_list_replenishment_slot_features_kernel(
             )
         tab_sb[0] = load_words(tab_words[0], "tab_sb0")
         load_stacked_scales(nc.sync, tab_scales, tab_scales_sb)
-        w1_raw[0, 0] = load_rows(w1[0:PASS, 0:PASS], "w1_raw00")
-        w1_raw[1, 0] = load_rows(w1[PASS : 2 * PASS, 0:PASS], "w1_raw10")
+        w1_raw[0, 0] = load_rows(w1[0:PASS, 0:PASS], stage[0])
         tab_sb[1] = load_words(tab_words[1], "tab_sb1")
-        w1_raw[0, 1] = load_rows(w1[0:PASS, PASS : 2 * PASS], "w1_raw01")
-        w1_raw[1, 1] = load_rows(w1[PASS : 2 * PASS, PASS : 2 * PASS], "w1_raw11")
-        nc.sync.dma_start(gain_sb[:], gain.rearrange("(b p t) -> p b t", b=2, t=4))
-        nc.sync.dma_start(w5_sb[:].bitcast(I32), w5_words.rearrange("a p c i -> p a (c i)").bitcast(I32))
-        nc.sync.dma_start(wg1_sb[:], wg1)
-        nc.sync.dma_start(w3_sb[:].bitcast(I32), w3_words.rearrange("a p c -> p a c").bitcast(I32))
-        offs3_sb = load_list(offs3, "offs3_sb")
-        load_page(0)
-        load_page(1)
-        offs2_sb = load_list(offs2, "offs2_sb")
-        tab2_sb = load_words(tab2_words[0], "tab2_sb")
-        load_stacked_scales(nc.sync, tab2_scales, tab2_scales_sb)
-        load_page(2)
-        load_page(3)
-        w2_raw = [load_rows(w2[:, 0:PASS], "w2_raw0")]
-        w2_raw.append(load_rows(w2[:, PASS : 2 * PASS], "w2_raw1"))
-        pos1_sb = load_list(pos1, "pos1_sb")
-        w4_raw = [load_rows(w4[a * PASS : (a + 1) * PASS, :], "w4_raw%d" % a) for a in range(2)]
-        nc.sync.dma_start(wg2_sb[:], wg2)
-        offs4_sb = load_list(offs4, "offs4_sb")
+        w1_raw[1, 0] = load_rows(w1[PASS : 2 * PASS, 0:PASS], stage[1])
+        w1_raw[0, 1] = load_rows(w1[0:PASS, PASS : 2 * PASS], stage[2])
+        w1_raw[1, 1] = load_rows(w1[PASS : 2 * PASS, PASS : 2 * PASS], stage[3])
 
         v_codes = [None, None]
         w1_q = {}
@@ -153,9 +137,29 @@ def tile_list_replenishment_slot_features_kernel(
         v_scales = gather(tab_scales_sb, offs_sb, U8, "v_scales")
         w1_q[0, 0] = quantize_held(interleave("scalar", w1_raw[0, 0], True, "w1_g00"), "w1_00")
         v_codes[1] = gather(tab_sb[1], offs_sb, U32, "v_codes1")
-        w1_q[1, 0] = quantize_held(interleave("scalar", w1_raw[1, 0], True, "w1_g10"), "w1_10")
-        w1_q[0, 1] = quantize_held(interleave("vector", w1_raw[0, 1], True, "w1_g01"), "w1_01")
-        w1_q[1, 1] = quantize_held(interleave("vector", w1_raw[1, 1], True, "w1_g11"), "w1_11")
+        w1_q[1, 0] = quantize_held(interleave("vector", w1_raw[1, 0], True, "w1_g10"), "w1_10")
+        w1_q[0, 1] = quantize_held(interleave("scalar", w1_raw[0, 1], True, "w1_g01"), "w1_01")
+        last_g = interleave("vector", w1_raw[1, 1], True, "w1_g11")
+        w1_q[1, 1] = quantize_held(last_g, "w1_11")
+
+        nc.gpsimd.dma_start(gain_sb[:], gain.rearrange("(b p t) -> p b t", b=2, t=4))
+        nc.sync.dma_start(w5_sb[:].bitcast(I32), w5_words.rearrange("a p c i -> p a (c i)").bitcast(I32))
+        nc.sync.dma_start(wg1_sb[:], wg1)
+        nc.sync.dma_start(w3_sb[:].bitcast(I32), w3_words.bitcast(I32).rearrange("a p c -> p a c"))
+        offs3_sb = load_list(offs3, "offs3_sb")
+        load_page(0)
+        load_page(1)
+        load_page(2)
+        w2_raw = [load_rows(w2[:, 0:PASS], stage[0])]
+        offs2_sb = load_list(offs2, "offs2_sb")
+        tab2_sb = load_words(tab2_words[0], "tab2_sb")
+        load_stacked_scales(nc.gpsimd, tab2_scales, tab2_scales_sb)
+        w2_raw.append(load_rows(w2[:, PASS : 2 * PASS], stage[1]))
+        pos1_sb = load_list(pos1, "pos1_sb")
+        load_page(3)
+        w4_raw = [load_rows(w4[a * PASS : (a + 1) * PASS, :], stage[2 + a]) for a in range(2)]
+        nc.sync.dma_start(wg2_sb[:], wg2)
+        offs4_sb = load_list(offs4, "offs4_sb")
 
         h1 = [[held([P, S], F32, "h1_%d%d" % (b, t)) for t in range(4)] for b in range(2)]
 
@@ -175,44 +179,52 @@ def tile_list_replenishment_slot_features_kernel(
         turn_banks = [psum.tile([P, 2, CHUNK], F32, name="turn_bank%d" % i) for i in range(2)]
         y_banks = [psum.tile([P, 2, CHUNK], F32, name="y_bank%d" % i) for i in range(2)]
 
-        def make_z1(c, b, work, z1_bf, gain_engine):
+        def make_h1(c, b, work=None):
             cols = slice(c * CHUNK, (c + 1) * CHUNK)
+            first = 2 * (c % 2 if c < 2 else b)
             for u in range(2):
-                bank = h_banks[2 * b + u]
+                bank = h_banks[first + u]
                 for e in range(2):
                     m_cols = slice((2 * u + e) * P, (2 * u + e + 1) * P)
                     times_v(bank[:, e, :], lambda a: w1_q[a, b][0][:, m_cols], lambda a: w1_q[a, b][1][:, m_cols], cols)
-                half = work[:, u * 2 * CHUNK : (u + 1) * 2 * CHUNK]
-                if gain_engine == "vector":
+                if work is not None:
+                    half = work[:, u * 2 * CHUNK : (u + 1) * 2 * CHUNK]
                     nc.scalar.activation(half.rearrange("p (n e) -> p n e", e=2), bank[:].rearrange("p e n -> p n e"), TANH)
-                else:
-                    nc.scalar.activation(half.rearrange("p (e n) -> p e n", e=2), bank[:], TANH)
-                for e in range(2):
-                    nc.scalar.copy(h1[b][2 * u + e][:, cols], bank[:, e, :])
-            if gain_engine == "vector":
-                nc.vector.tensor_tensor(
-                    z1_bf.rearrange("p (n u e) -> p n u e", u=2, e=2),
-                    work[:].rearrange("p (u n e) -> p n u e", u=2, e=2),
-                    gain_sb[:, b, :].rearrange("p (u e) -> p u e", u=2).unsqueeze(1).to_broadcast([P, CHUNK, 2, 2]),
-                    MULT,
-                )
-            else:
-                planes = ring.tile([P, 4, CHUNK], BF16, name="planes", bufs=2)
-                for t in range(4):
-                    nc.scalar.activation(
-                        planes[:, t, :], work[:, t * CHUNK : (t + 1) * CHUNK], COPY, scale=gain_sb[:, b, t : t + 1]
-                    )
-                nc.scalar.copy(
-                    z1_bf.rearrange("p (c i j) -> p c j i", i=4, j=4), planes[:].rearrange("p j (c i) -> p c j i", i=4)
-                )
+            for t in range(4):
+                nc.scalar.copy(h1[b][t][:, cols], h_banks[first + t // 2][:, t % 2, :])
+
+        def quantize_z1(z1_bf):
             codes = ring.tile([P, CHUNK], U32, name="z1_codes", bufs=4, align_bytes=64)
             scales = ring.tile([P, CHUNK], U8, name="z1_scales", bufs=4, align_bytes=64)
             nc.vector.quantize_mx(out=codes[:].bitcast(FP8X4), scales=scales[:], in_=z1_bf)
             return codes, scales
 
-        def make_factor(c, pair, factor):
+        def z1_by_vector(c, b, work, z1_bf):
+            make_h1(c, b, work)
+            nc.vector.tensor_tensor(
+                z1_bf.rearrange("p (n u e) -> p n u e", u=2, e=2),
+                work[:].rearrange("p (u n e) -> p n u e", u=2, e=2),
+                gain_sb[:, b, :].rearrange("p (u e) -> p u e", u=2).unsqueeze(1).to_broadcast([P, CHUNK, 2, 2]),
+                MULT,
+            )
+            return quantize_z1(z1_bf)
+
+        def z1_by_scalar(c, b, work, z1_bf, spare):
             cols = slice(c * CHUNK, (c + 1) * CHUNK)
-            bank = turn_banks[pair]
+            planes = spare[:].bitcast(BF16).rearrange("p (t n) -> p t n", t=4)
+            for t in range(4):
+                nc.scalar.activation(work[:, t * CHUNK : (t + 1) * CHUNK], h1[b][t][:, cols], TANH)
+            for t in range(4):
+                nc.scalar.activation(
+                    planes[:, t, :], work[:, t * CHUNK : (t + 1) * CHUNK], COPY, scale=gain_sb[:, b, t : t + 1]
+                )
+            nc.scalar.copy(
+                z1_bf.rearrange("p (c i j) -> p c j i", i=4, j=4), planes.rearrange("p j (c i) -> p c j i", i=4)
+            )
+            return quantize_z1(z1_bf)
+
+        def make_factor(c, pair, factor, bank):
+            cols = slice(c * CHUNK, (c + 1) * CHUNK)
             for i in range(2):
                 m_cols = slice((2 * pair + i) * P, (2 * pair + i + 1) * P)
                 times_v(bank[:, i, :], lambda a: w5_sb[:, a, m_cols], lambda a: w5_scales_sb[4 * a :, m_cols], cols)
@@ -224,9 +236,9 @@ def tile_list_replenishment_slot_features_kernel(
             )
             return factor
 
-        def make_y1(z1_q, y1_sb):
+        def make_y1(z1_q, y1_sb, banks):
             for pair in range(2):
-                bank = y_banks[pair]
+                bank = banks[pair]
                 for i in range(2):
                     nt = 2 * pair + i
                     for a in range(2):
@@ -244,9 +256,9 @@ def tile_list_replenishment_slot_features_kernel(
                 )
             return y1_sb
 
-        def put_y1(c, pair, y1_sb, factor):
+        def put_y1(c, pair, y1_sb, factor, which=(0, 1)):
             places = offs3_sb[:, c * CHUNK // 16 : (c + 1) * CHUNK // 16]
-            for i in range(2):
+            for i in which:
                 nt = 2 * pair + i
                 nc.vector.tensor_tensor(
                     pages[nt][:].indirect(places),
@@ -256,7 +268,7 @@ def tile_list_replenishment_slot_features_kernel(
                 )
 
         def make_h2(w2_q, v2_codes, v2_scales):
-            h2_sb = ring.tile([P, 4, PASS], F32, name="h2_sb", tag="raw", bufs=5)
+            h2_sb = ring.tile([P, 4, PASS], F32, name="h2_sb", tag="wide", bufs=3, align_bytes=64)
             for t in range(4):
                 m_cols = slice(t * P, (t + 1) * P)
                 bank = h_banks[t][:].rearrange("p e n -> p (e n)")
@@ -272,13 +284,12 @@ def tile_list_replenishment_slot_features_kernel(
                 nc.scalar.copy(h2_sb[:, t, :], bank)
             return h2_sb
 
-        def join(h2_sb, b):
-            z2_f = ring.tile([P, 4, PASS], F32, name="z2_f", tag="raw", bufs=5)
-            for t in range(4):
+        def join(h2_sb, b, z2_f, planes_wanted):
+            for t in planes_wanted:
                 nc.vector.tensor_tensor(z2_f[:, t, :], h1[b][t][:].indirect(pos1_sb[:]), h2_sb[:, t, :], MULT)
-            return interleave("scalar", z2_f, False, "z2_g")
 
-        work = [held([P, 4 * CHUNK], F32, "work%d" % i) for i in range(4)]
+        work = [held([P, 4 * CHUNK], F32, "work%d" % i) for i in range(5)]
+        spare = [held([P, 2 * CHUNK], F32, "spare%d" % i) for i in range(4)]
         gate = [held([P, 2 * CHUNK], F32, "gate%d" % i) for i in range(2)]
 
         def fresh_bf():
@@ -286,43 +297,48 @@ def tile_list_replenishment_slot_features_kernel(
             return tile[:]
 
         def fresh_factor():
-            tile = ring.tile([P, 2 * CHUNK], F32, name="factor", bufs=2)
+            tile = ring.tile([P, 2 * CHUNK], F32, name="factor", bufs=4)
             return tile[:]
 
-        z00 = make_z1(0, 0, work[0], fresh_bf(), "vector")
-        z01 = make_z1(0, 1, work[2], gate[0][:].bitcast(BF16), "vector")
-        f00 = make_factor(0, 0, fresh_factor())
-        y0 = make_y1([z00, z01], work[3])
+        z00 = z1_by_vector(0, 0, work[0], last_g[:, 0 : 4 * CHUNK])
+        z01 = z1_by_vector(0, 1, work[2], fresh_bf())
+        f00 = make_factor(0, 0, fresh_factor(), turn_banks[0])
+        f01 = make_factor(0, 1, fresh_factor(), turn_banks[1])
+        y0 = make_y1([z00, z01], work[3], y_banks)
         put_y1(0, 0, y0, f00)
-        z10 = make_z1(1, 0, work[1], fresh_bf(), "vector")
-        z11 = make_z1(1, 1, work[0], gate[1][:].bitcast(BF16), "vector")
-        put_y1(0, 1, y0, make_factor(0, 1, gate[1][:]))
-        f10 = make_factor(1, 0, fresh_factor())
-        z20 = make_z1(2, 0, work[1], fresh_bf(), "scalar")
-        y1 = make_y1([z10, z11], work[1])
+        z10 = z1_by_vector(1, 0, work[1], fresh_bf())
+        z11 = z1_by_vector(1, 1, work[0], fresh_bf())
+        f10 = make_factor(1, 0, fresh_factor(), turn_banks[0])
+        f11 = make_factor(1, 1, fresh_factor(), turn_banks[1])
+        for c in (2, 3):
+            for b in range(2):
+                make_h1(c, b)
+        y1 = make_y1([z10, z11], work[4], h_banks[2:])
         put_y1(1, 0, y1, f10)
+        put_y1(0, 1, y0, f01)
+        put_y1(1, 1, y1, f11)
         v2_codes = gather(tab2_sb, offs2_sb, U32, "v2_codes")
         v2_scales = gather(tab2_scales_sb, offs2_sb, U8, "v2_scales")
-        z21 = make_z1(2, 1, work[2], gate[0][:].bitcast(BF16), "scalar")
-        put_y1(1, 1, y1, make_factor(1, 1, gate[0][:]))
-        f20 = make_factor(2, 0, fresh_factor())
-        w2_g = [interleave("scalar", w2_raw[b], True, "w2_g") for b in range(2)]
-        w2_q = [quantize_held(w2_g[b], "w2_%d" % b) for b in range(2)]
-        z30 = make_z1(3, 0, work[0], fresh_bf(), "scalar")
-        y2 = make_y1([z20, z21], work[0])
-        put_y1(2, 0, y2, f20)
-        z31 = make_z1(3, 1, work[2], gate[1][:].bitcast(BF16), "vector")
-        put_y1(2, 1, y2, make_factor(2, 1, gate[1][:]))
-        h2_sb = [make_h2(w2_q[b], v2_codes, v2_scales) for b in range(2)]
-        y3 = make_y1([z30, z31], work[3])
+        w2_q = [quantize_held(interleave("scalar", w2_raw[b], True, "w2_g"), "w2_%d" % b) for b in range(2)]
+        z2_f = [stage[0], stage[1]]
+        z20 = z1_by_scalar(2, 0, work[0], fresh_bf(), spare[0])
+        h2_sb = [make_h2(w2_q[0], v2_codes, v2_scales)]
+        join(h2_sb[0], 0, z2_f[0], range(4))
+        z21 = z1_by_scalar(2, 1, work[2], z2_f[1][:, 2, :].bitcast(BF16), spare[1])
+        h2_sb.append(make_h2(w2_q[1], v2_codes, v2_scales))
+        join(h2_sb[1], 1, z2_f[1], range(4))
+        y2 = make_y1([z20, z21], work[0], y_banks)
+        put_y1(2, 0, y2, make_factor(2, 0, h2_sb[1][:, 3, :], h_banks[0]))
+        z2_g = [interleave("scalar", z2_f[0], False, "z2_g", work[2][:].bitcast(BF16))]
         w4_q = [quantize_held(interleave("scalar", w4_raw[a], False, "w4_g"), "w4_%d" % a) for a in range(2)]
-        z2_g = [join(h2_sb[b], b) for b in range(2)]
-        put_y1(3, 0, y3, make_factor(3, 0, h2_sb[1][:, 3, :]))
+        last_stage = stage[3][:].rearrange("p j c -> p (j c)")
+        z2_g.append(interleave("scalar", z2_f[1], False, "z2_g", last_stage[:, 0 : 2 * PASS].bitcast(BF16)))
         z2_q = [quantize_held(z2_g[b], "z2_%d" % b) for b in range(2)]
-        put_y1(3, 1, y3, make_factor(3, 1, z2_g[1][:, 0 : 4 * CHUNK].bitcast(F32)))
-        for nt in range(N // P):
+        put_y1(2, 1, y2, make_factor(2, 1, last_stage[:, 0 : 2 * CHUNK], h_banks[1]))
+
+        def put_y2(nt, y2_sb):
             m_cols = slice(nt * P, (nt + 1) * P)
-            bank = h_banks[nt][:].rearrange("p e n -> p (e n)")
+            bank = h_banks[(nt + 2) % 4][:].rearrange("p e n -> p (e n)")
             for a in range(2):
                 nc.tensor.matmul_mx(
                     out=bank,
@@ -333,7 +349,17 @@ def tile_list_replenishment_slot_features_kernel(
                     start=(a == 0),
                     stop=(a == 1),
                 )
-            y2_sb = ring.tile([P, P2], F32, name="y2_sb", bufs=2)
             nc.scalar.copy(y2_sb[:], bank)
             nc.vector.tensor_tensor(pages[nt][:].indirect(offs4_sb[:]), y2_sb[:], wg2_sb[:], MULT)
-            nc.sync.dma_start(out[m_cols, :], pages[nt][:])
+
+        put_y2(0, spare[0])
+        put_y2(1, spare[1])
+        z30 = z1_by_scalar(3, 0, stage[1][:].rearrange("p j c -> p (j c)"), fresh_bf(), spare[2])
+        z31 = z1_by_scalar(3, 1, stage[1][:].rearrange("p j c -> p (j c)")[:, 4 * CHUNK :], fresh_bf(), spare[3])
+        put_y2(2, spare[3])
+        y3 = make_y1([z30, z31], work[1], turn_banks)
+        put_y1(3, 0, y3, make_factor(3, 0, fresh_factor(), y_banks[0]))
+        put_y1(3, 1, y3, make_factor(3, 1, fresh_factor(), y_banks[1]))
+        put_y2(3, spare[2])
+        for nt in range(N // P):
+            nc.sync.dma_start(out[nt * P : (nt + 1) * P, :], pages[nt][:])

@@ -73,7 +73,14 @@ def tile_list_replenishment_slot_features_kernel(
         def interleave(engine, raw, deal_columns, name, grouped=None):
             if grouped is None:
                 grouped = ring.tile([P, 4 * PASS], BF16, name=name, tag="grouped", bufs=3, align_bytes=64)
-            if deal_columns:
+            if engine == "both":
+                for half, name_of_engine in enumerate(("vector", "scalar")):
+                    copy_on(
+                        name_of_engine,
+                        grouped[:, half * 2 * PASS : (half + 1) * 2 * PASS].rearrange("p (t m j) -> p m j t", t=2, j=4),
+                        raw[:].rearrange("p j (m t) -> p m j t", t=4)[:, :, :, 2 * half : 2 * half + 2],
+                    )
+            elif deal_columns:
                 copy_on(
                     engine,
                     grouped[:].rearrange("p (t m j) -> p m j t", t=4, j=4),
@@ -137,12 +144,12 @@ def tile_list_replenishment_slot_features_kernel(
         v_scales = gather(tab_scales_sb, offs_sb, U8, "v_scales")
         w1_q[0, 0] = quantize_held(interleave("scalar", w1_raw[0, 0], True, "w1_g00"), "w1_00")
         v_codes[1] = gather(tab_sb[1], offs_sb, U32, "v_codes1")
-        w1_q[1, 0] = quantize_held(interleave("vector", w1_raw[1, 0], True, "w1_g10"), "w1_10")
-        w1_q[0, 1] = quantize_held(interleave("scalar", w1_raw[0, 1], True, "w1_g01"), "w1_01")
-        last_g = interleave("vector", w1_raw[1, 1], True, "w1_g11")
+        w1_q[1, 0] = quantize_held(interleave("both", w1_raw[1, 0], True, "w1_g10"), "w1_10")
+        w1_q[0, 1] = quantize_held(interleave("both", w1_raw[0, 1], True, "w1_g01"), "w1_01")
+        last_g = interleave("both", w1_raw[1, 1], True, "w1_g11")
         w1_q[1, 1] = quantize_held(last_g, "w1_11")
 
-        nc.gpsimd.dma_start(gain_sb[:], gain.rearrange("(b p t) -> p b t", b=2, t=4))
+        nc.sync.dma_start(gain_sb[:], gain.rearrange("(b p t) -> p b t", b=2, t=4))
         nc.sync.dma_start(w5_sb[:].bitcast(I32), w5_words.rearrange("a p c i -> p a (c i)").bitcast(I32))
         nc.sync.dma_start(wg1_sb[:], wg1)
         nc.sync.dma_start(w3_sb[:].bitcast(I32), w3_words.bitcast(I32).rearrange("a p c -> p a c"))
@@ -153,7 +160,7 @@ def tile_list_replenishment_slot_features_kernel(
         w2_raw = [load_rows(w2[:, 0:PASS], stage[0])]
         offs2_sb = load_list(offs2, "offs2_sb")
         tab2_sb = load_words(tab2_words[0], "tab2_sb")
-        load_stacked_scales(nc.gpsimd, tab2_scales, tab2_scales_sb)
+        load_stacked_scales(nc.sync, tab2_scales, tab2_scales_sb)
         w2_raw.append(load_rows(w2[:, PASS : 2 * PASS], stage[1]))
         pos1_sb = load_list(pos1, "pos1_sb")
         load_page(3)
@@ -176,12 +183,14 @@ def tile_list_replenishment_slot_features_kernel(
                 )
 
         h_banks = [psum.tile([P, 2, CHUNK], F32, name="h_bank%d" % i) for i in range(4)]
+        first_banks = h_banks
         turn_banks = [psum.tile([P, 2, CHUNK], F32, name="turn_bank%d" % i) for i in range(2)]
         y_banks = [psum.tile([P, 2, CHUNK], F32, name="y_bank%d" % i) for i in range(2)]
 
         def make_h1(c, b, work=None):
+            h_banks = (y_banks + y_banks) if c == 1 else first_banks
             cols = slice(c * CHUNK, (c + 1) * CHUNK)
-            first = 2 * (c % 2 if c < 2 else b)
+            first = 2 * (b)
             for u in range(2):
                 bank = h_banks[first + u]
                 for e in range(2):
@@ -256,6 +265,21 @@ def tile_list_replenishment_slot_features_kernel(
                 )
             return y1_sb
 
+        def make_first_y1(z1_q, y1_sb):
+            for nt in range(4):
+                for a in range(2):
+                    nc.tensor.matmul_mx(
+                        out=h_banks[nt][:, 0, :],
+                        lhsT=w3_sb[:, a, 2 * nt * P : 2 * (nt + 1) * P].bitcast(FP4X4),
+                        lhsT_scale=w3_scales_sb[:, a, nt * P : (nt + 1) * P],
+                        rhs=z1_q[a][0][:].bitcast(FP8X4),
+                        rhs_scale=z1_q[a][1][:],
+                        start=(a == 0),
+                        stop=(a == 1),
+                    )
+                nc.scalar.copy(y1_sb[:, nt * CHUNK : (nt + 1) * CHUNK], h_banks[nt][:, 0, :])
+            return y1_sb
+
         def put_y1(c, pair, y1_sb, factor, which=(0, 1)):
             places = offs3_sb[:, c * CHUNK // 16 : (c + 1) * CHUNK // 16]
             for i in which:
@@ -290,7 +314,6 @@ def tile_list_replenishment_slot_features_kernel(
 
         work = [held([P, 4 * CHUNK], F32, "work%d" % i) for i in range(5)]
         spare = [held([P, 2 * CHUNK], F32, "spare%d" % i) for i in range(4)]
-        gate = [held([P, 2 * CHUNK], F32, "gate%d" % i) for i in range(2)]
 
         def fresh_bf():
             tile = ring.tile([P, 4 * CHUNK], BF16, name="z1_bf", bufs=2, align_bytes=64)
@@ -304,22 +327,24 @@ def tile_list_replenishment_slot_features_kernel(
         z01 = z1_by_vector(0, 1, work[2], fresh_bf())
         f00 = make_factor(0, 0, fresh_factor(), turn_banks[0])
         f01 = make_factor(0, 1, fresh_factor(), turn_banks[1])
-        y0 = make_y1([z00, z01], work[3], y_banks)
+        y0 = make_first_y1([z00, z01], work[3])
         put_y1(0, 0, y0, f00)
-        z10 = z1_by_vector(1, 0, work[1], fresh_bf())
-        z11 = z1_by_vector(1, 1, work[0], fresh_bf())
+        z10 = z1_by_vector(1, 0, work[0], fresh_bf())
+        shared_g = held([P, 4 * PASS], BF16, "shared_g")
+        z11 = z1_by_vector(1, 1, work[1], shared_g[:, 0 : 4 * CHUNK])
         f10 = make_factor(1, 0, fresh_factor(), turn_banks[0])
         f11 = make_factor(1, 1, fresh_factor(), turn_banks[1])
+        y1 = make_y1([z10, z11], work[4], y_banks)
         for c in (2, 3):
             for b in range(2):
                 make_h1(c, b)
-        y1 = make_y1([z10, z11], work[4], h_banks[2:])
         put_y1(1, 0, y1, f10)
         put_y1(0, 1, y0, f01)
         put_y1(1, 1, y1, f11)
         v2_codes = gather(tab2_sb, offs2_sb, U32, "v2_codes")
         v2_scales = gather(tab2_scales_sb, offs2_sb, U8, "v2_scales")
-        w2_q = [quantize_held(interleave("scalar", w2_raw[b], True, "w2_g"), "w2_%d" % b) for b in range(2)]
+        w2_q = [quantize_held(interleave("scalar", w2_raw[0], True, "w2_g", shared_g), "w2_0")]
+        w2_q.append(quantize_held(interleave("scalar", w2_raw[1], True, "w2_g"), "w2_1"))
         z2_f = [stage[0], stage[1]]
         z20 = z1_by_scalar(2, 0, work[0], fresh_bf(), spare[0])
         h2_sb = [make_h2(w2_q[0], v2_codes, v2_scales)]

from contextlib import ExitStack

import concourse.mybir as mybir

K, K2, H, N, T, S, P2, T2 = 1024, 512, 1024, 512, 2048, 1024, 512, 2048
FLOPS = 2 * (K * H * S + K2 * H * P2 + K * N * S + H * N * S + H * N * P2)

F32 = mybir.dt.float32
BF16 = mybir.dt.bfloat16
I32 = mybir.dt.int32
U32 = mybir.dt.uint32
U16 = mybir.dt.uint16
U8 = mybir.dt.uint8
FP8X4 = mybir.dt.float8_e4m3fn_x4
FP4X4 = mybir.dt.float4_e2m1fn_x4
MULT = mybir.AluOpType.mult
COPY = mybir.ActivationFunctionType.Copy
TANH = mybir.ActivationFunctionType.Tanh

P = 128
PASS = 512
CHUNK = 256


def tile_list_replenishment_slot_features_kernel(
    tc, tab_words, tab_scales, tab2_words, tab2_scales, offs, offs2, pos1, offs3, offs4,
    w1, w2, w3_words, w3_scales, w4, w5_words, w5_scales, gain, page1, wg1, wg2, out,
):
    nc = tc.nc
    with ExitStack() as ctx:
        keep = ctx.enter_context(tc.tile_pool(name="keep", bufs=1))
        ring = ctx.enter_context(tc.tile_pool(name="ring", bufs=2))
        psum = ctx.enter_context(tc.psum_pool(name="psum", bufs=1))

        def held(shape, dtype, name):
            return keep.tile(shape, dtype, name=name, align_bytes=64)

        def load_list(src, name):
            tile = keep.tile(list(src.shape), U16, name=name)
            nc.sync.dma_start(tile[:], src)
            return tile

        def load_words(src, name):
            tile = ring.tile([P, src.shape[1]], U32, name=name, tag="wide", bufs=3, align_bytes=64)
            nc.sync.dma_start(tile[:].bitcast(I32), src.rearrange("p t i -> p (t i)").bitcast(I32))
            return tile

        def load_stacked_scales(queue, src, tile):
            passes = src.shape[0]
            for q in range(4):
                queue.dma_start(
                    tile[32 * q : 32 * q + 4 * passes, :].bitcast(I32),
                    src[:, 4 * q : 4 * q + 4, :].bitcast(I32),
                )

        def zeroed(width, name):
            tile = held([P, width], U8, name)
            nc.vector.memset(tile[:].bitcast(I32), 0)
            return tile

        stage = [held([P, 4, PASS], F32, "stage%d" % i) for i in range(4)]

        def load_rows(rows, raw):
            nc.sync.dma_start(raw[:], rows.rearrange("(p j) c -> p j c", j=4))
            return raw

        def copy_on(engine, dst, src):
            if engine == "vector":
                nc.vector.tensor_copy(dst, src)
            else:
                nc.scalar.copy(dst, src)

        def interleave(engine, raw, deal_columns, name, grouped=None):
            if grouped is None:
                grouped = ring.tile([P, 4 * PASS], BF16, name=name, tag="grouped", bufs=3, align_bytes=64)
            if engine == "both":
                for half, name_of_engine in enumerate(("vector", "scalar")):
                    copy_on(
                        name_of_engine,
                        grouped[:, half * 2 * PASS : (half + 1) * 2 * PASS].rearrange("p (t m j) -> p m j t", t=2, j=4),
                        raw[:].rearrange("p j (m t) -> p m j t", t=4)[:, :, :, 2 * half : 2 * half + 2],
                    )
            elif deal_columns:
                copy_on(
                    engine,
                    grouped[:].rearrange("p (t m j) -> p m j t", t=4, j=4),
                    raw[:].rearrange("p j (m t) -> p m j t", t=4),
                )
            else:
                copy_on(
                    engine,
                    grouped[:].rearrange("p (c i j) -> p c j i", i=4, j=4),
                    raw[:].rearrange("p j (c i) -> p c j i", i=4),
                )
            return grouped

        def quantize(grouped, codes, scales):
            nc.vector.quantize_mx(out=codes[:].bitcast(FP8X4), scales=scales[:], in_=grouped[:])
            return codes, scales

        def quantize_held(grouped, name):
            return quantize(grouped, held([P, PASS], U32, name + "_codes"), held([P, PASS], U8, name + "_scales"))

        def gather(window, offsets, dtype, name):
            picked = held([P, 16 * offsets.shape[1]], dtype, name)
            nc.vector.tensor_copy(picked[:], window[:].indirect(offsets[:]))
            return picked

        offs_sb = load_list(offs, "offs_sb")
        tab_scales_sb = zeroed(T, "tab_scales_sb")
        w5_scales_sb = zeroed(N, "w5_scales_sb")
        w3_scales_flat = zeroed(2 * N, "w3_scales_sb")
        w3_scales_sb = w3_scales_flat[:].rearrange("p (a c) -> p a c", a=2)
        tab2_scales_sb = zeroed(T, "tab2_scales_sb")
        tab_sb = [None, None]
        w1_raw = {}
        gain_sb = held([P, 2, 4], F32, "gain_sb")
        w5_sb = held([P, 2, N], U32, "w5_sb")
        wg1_sb = held([P, S], F32, "wg1_sb")
        w3_sb = held([P, 2, 2 * N], U8, "w3_sb")
        wg2_sb = held([P, P2], F32, "wg2_sb")
        pages = [held([P, T2], F32, "page%d" % nt) for nt in range(N // P)]

        def load_page(nt):
            nc.sync.dma_start(pages[nt][:], page1[nt * P : (nt + 1) * P, :])

        load_stacked_scales(nc.gpsimd, w5_scales, w5_scales_sb)
        for q in range(4):
            nc.gpsimd.dma_start(
                w3_scales_sb[32 * q : 32 * q + 4, :, :].bitcast(I32),
                w3_scales[:, 4 * q : 4 * q + 4, :].rearrange("a r c -> r a c").bitcast(I32),
            )
        tab_sb[0] = load_words(tab_words[0], "tab_sb0")
        load_stacked_scales(nc.sync, tab_scales, tab_scales_sb)
        w1_raw[0, 0] = load_rows(w1[0:PASS, 0:PASS], stage[0])
        tab_sb[1] = load_words(tab_words[1], "tab_sb1")
        w1_raw[1, 0] = load_rows(w1[PASS : 2 * PASS, 0:PASS], stage[1])
        w1_raw[0, 1] = load_rows(w1[0:PASS, PASS : 2 * PASS], stage[2])
        w1_raw[1, 1] = load_rows(w1[PASS : 2 * PASS, PASS : 2 * PASS], stage[3])

        v_codes = [None, None]
        w1_q = {}
        v_codes[0] = gather(tab_sb[0], offs_sb, U32, "v_codes0")
        v_scales = gather(tab_scales_sb, offs_sb, U8, "v_scales")
        w1_q[0, 0] = quantize_held(interleave("scalar", w1_raw[0, 0], True, "w1_g00"), "w1_00")
        v_codes[1] = gather(tab_sb[1], offs_sb, U32, "v_codes1")
        w1_q[1, 0] = quantize_held(interleave("both", w1_raw[1, 0], True, "w1_g10"), "w1_10")
        w1_q[0, 1] = quantize_held(interleave("both", w1_raw[0, 1], True, "w1_g01"), "w1_01")
        last_g = interleave("both", w1_raw[1, 1], True, "w1_g11")
        w1_q[1, 1] = quantize_held(last_g, "w1_11")

        nc.sync.dma_start(gain_sb[:], gain.rearrange("(b p t) -> p b t", b=2, t=4))
        nc.sync.dma_start(w5_sb[:].bitcast(I32), w5_words.rearrange("a p c i -> p a (c i)").bitcast(I32))
        nc.sync.dma_start(wg1_sb[:], wg1)
        nc.sync.dma_start(w3_sb[:].bitcast(I32), w3_words.bitcast(I32).rearrange("a p c -> p a c"))
        offs3_sb = load_list(offs3, "offs3_sb")
        load_page(0)
        load_page(1)
        load_page(2)
        w2_raw = [load_rows(w2[:, 0:PASS], stage[0])]
        offs2_sb = load_list(offs2, "offs2_sb")
        tab2_sb = load_words(tab2_words[0], "tab2_sb")
        load_stacked_scales(nc.sync, tab2_scales, tab2_scales_sb)
        w2_raw.append(load_rows(w2[:, PASS : 2 * PASS], stage[1]))
        pos1_sb = load_list(pos1, "pos1_sb")
        load_page(3)
        w4_raw = [load_rows(w4[a * PASS : (a + 1) * PASS, :], stage[2 + a]) for a in range(2)]
        nc.sync.dma_start(wg2_sb[:], wg2)
        offs4_sb = load_list(offs4, "offs4_sb")

        h1 = [[held([P, S], F32, "h1_%d%d" % (b, t)) for t in range(4)] for b in range(2)]

        def times_v(acc, codes_of, scales_of, cols):
            for a in range(2):
                nc.tensor.matmul_mx(
                    out=acc,
                    lhsT=codes_of(a).bitcast(FP8X4),
                    lhsT_scale=scales_of(a),
                    rhs=v_codes[a][:, cols].bitcast(FP8X4),
                    rhs_scale=v_scales[4 * a :, cols],
                    start=(a == 0),
                    stop=(a == 1),
                )

        h_banks = [psum.tile([P, 2, CHUNK], F32, name="h_bank%d" % i) for i in range(4)]
        first_banks = h_banks
        turn_banks = [psum.tile([P, 2, CHUNK], F32, name="turn_bank%d" % i) for i in range(2)]
        y_banks = [psum.tile([P, 2, CHUNK], F32, name="y_bank%d" % i) for i in range(2)]

        def make_h1(c, b, work=None):
            h_banks = (y_banks + y_banks) if c == 1 else first_banks
            cols = slice(c * CHUNK, (c + 1) * CHUNK)
            first = 2 * (b)
            for u in range(2):
                bank = h_banks[first + u]
                for e in range(2):
                    m_cols = slice((2 * u + e) * P, (2 * u + e + 1) * P)
                    times_v(bank[:, e, :], lambda a: w1_q[a, b][0][:, m_cols], lambda a: w1_q[a, b][1][:, m_cols], cols)
                if work is not None:
                    half = work[:, u * 2 * CHUNK : (u + 1) * 2 * CHUNK]
                    nc.scalar.activation(half.rearrange("p (n e) -> p n e", e=2), bank[:].rearrange("p e n -> p n e"), TANH)
            for t in range(4):
                nc.scalar.copy(h1[b][t][:, cols], h_banks[first + t // 2][:, t % 2, :])

        def quantize_z1(z1_bf):
            codes = ring.tile([P, CHUNK], U32, name="z1_codes", bufs=4, align_bytes=64)
            scales = ring.tile([P, CHUNK], U8, name="z1_scales", bufs=4, align_bytes=64)
            nc.vector.quantize_mx(out=codes[:].bitcast(FP8X4), scales=scales[:], in_=z1_bf)
            return codes, scales

        def z1_by_vector(c, b, work, z1_bf):
            make_h1(c, b, work)
            nc.vector.tensor_tensor(
                z1_bf.rearrange("p (n u e) -> p n u e", u=2, e=2),
                work[:].rearrange("p (u n e) -> p n u e", u=2, e=2),
                gain_sb[:, b, :].rearrange("p (u e) -> p u e", u=2).unsqueeze(1).to_broadcast([P, CHUNK, 2, 2]),
                MULT,
            )
            return quantize_z1(z1_bf)

        def z1_by_scalar(c, b, work, z1_bf, spare):
            cols = slice(c * CHUNK, (c + 1) * CHUNK)
            planes = spare[:].bitcast(BF16).rearrange("p (t n) -> p t n", t=4)
            for t in range(4):
                nc.scalar.activation(work[:, t * CHUNK : (t + 1) * CHUNK], h1[b][t][:, cols], TANH)
            for t in range(4):
                nc.scalar.activation(
                    planes[:, t, :], work[:, t * CHUNK : (t + 1) * CHUNK], COPY, scale=gain_sb[:, b, t : t + 1]
                )
            nc.scalar.copy(
                z1_bf.rearrange("p (c i j) -> p c j i", i=4, j=4), planes.rearrange("p j (c i) -> p c j i", i=4)
            )
            return quantize_z1(z1_bf)

        def make_factor(c, pair, factor, bank):
            cols = slice(c * CHUNK, (c + 1) * CHUNK)
            for i in range(2):
                m_cols = slice((2 * pair + i) * P, (2 * pair + i + 1) * P)
                times_v(bank[:, i, :], lambda a: w5_sb[:, a, m_cols], lambda a: w5_scales_sb[4 * a :, m_cols], cols)
            nc.vector.tensor_tensor(
                factor.rearrange("p (i n) -> p i n", i=2),
                bank[:],
                wg1_sb[:, cols].unsqueeze(1).to_broadcast([P, 2, CHUNK]),
                MULT,
            )
            return factor

        def make_y1(z1_q, y1_sb, banks):
            for pair in range(2):
                bank = banks[pair]
                for i in range(2):
                    nt = 2 * pair + i
                    for a in range(2):
                        nc.tensor.matmul_mx(
                            out=bank[:, i, :],
                            lhsT=w3_sb[:, a, 2 * nt * P : 2 * (nt + 1) * P].bitcast(FP4X4),
                            lhsT_scale=w3_scales_sb[:, a, nt * P : (nt + 1) * P],
                            rhs=z1_q[a][0][:].bitcast(FP8X4),
                            rhs_scale=z1_q[a][1][:],
                            start=(a == 0),
                            stop=(a == 1),
                        )
                nc.scalar.copy(
                    y1_sb[:, pair * 2 * CHUNK : (pair + 1) * 2 * CHUNK].rearrange("p (i n) -> p i n", i=2), bank[:]
                )
            return y1_sb

        def make_first_y1(z1_q, y1_sb):
            for nt in range(4):
                for a in range(2):
                    nc.tensor.matmul_mx(
                        out=h_banks[nt][:, 0, :],
                        lhsT=w3_sb[:, a, 2 * nt * P : 2 * (nt + 1) * P].bitcast(FP4X4),
                        lhsT_scale=w3_scales_sb[:, a, nt * P : (nt + 1) * P],
                        rhs=z1_q[a][0][:].bitcast(FP8X4),
                        rhs_scale=z1_q[a][1][:],
                        start=(a == 0),
                        stop=(a == 1),
                    )
                nc.scalar.copy(y1_sb[:, nt * CHUNK : (nt + 1) * CHUNK], h_banks[nt][:, 0, :])
            return y1_sb

        def put_y1(c, pair, y1_sb, factor, which=(0, 1)):
            places = offs3_sb[:, c * CHUNK // 16 : (c + 1) * CHUNK // 16]
            for i in which:
                nt = 2 * pair + i
                nc.vector.tensor_tensor(
                    pages[nt][:].indirect(places),
                    y1_sb[:, nt * CHUNK : (nt + 1) * CHUNK],
                    factor[:, i * CHUNK : (i + 1) * CHUNK],
                    MULT,
                )

        def make_h2(w2_q, v2_codes, v2_scales):
            h2_sb = ring.tile([P, 4, PASS], F32, name="h2_sb", tag="wide", bufs=3, align_bytes=64)
            for t in range(4):
                m_cols = slice(t * P, (t + 1) * P)
                bank = h_banks[t][:].rearrange("p e n -> p (e n)")
                nc.tensor.matmul_mx(
                    out=bank,
                    lhsT=w2_q[0][:, m_cols].bitcast(FP8X4),
                    lhsT_scale=w2_q[1][:, m_cols],
                    rhs=v2_codes[:].bitcast(FP8X4),
                    rhs_scale=v2_scales[:],
                    start=True,
                    stop=True,
                )
                nc.scalar.copy(h2_sb[:, t, :], bank)
            return h2_sb

        def join(h2_sb, b, z2_f, planes_wanted):
            for t in planes_wanted:
                nc.vector.tensor_tensor(z2_f[:, t, :], h1[b][t][:].indirect(pos1_sb[:]), h2_sb[:, t, :], MULT)

        work = [held([P, 4 * CHUNK], F32, "work%d" % i) for i in range(5)]
        spare = [held([P, 2 * CHUNK], F32, "spare%d" % i) for i in range(4)]

        def fresh_bf():
            tile = ring.tile([P, 4 * CHUNK], BF16, name="z1_bf", bufs=2, align_bytes=64)
            return tile[:]

        def fresh_factor():
            tile = ring.tile([P, 2 * CHUNK], F32, name="factor", bufs=4)
            return tile[:]

        z00 = z1_by_vector(0, 0, work[0], last_g[:, 0 : 4 * CHUNK])
        z01 = z1_by_vector(0, 1, work[2], fresh_bf())
        f00 = make_factor(0, 0, fresh_factor(), turn_banks[0])
        f01 = make_factor(0, 1, fresh_factor(), turn_banks[1])
        y0 = make_first_y1([z00, z01], work[3])
        put_y1(0, 0, y0, f00)
        z10 = z1_by_vector(1, 0, work[0], fresh_bf())
        shared_g = held([P, 4 * PASS], BF16, "shared_g")
        z11 = z1_by_vector(1, 1, work[1], shared_g[:, 0 : 4 * CHUNK])
        f10 = make_factor(1, 0, fresh_factor(), turn_banks[0])
        f11 = make_factor(1, 1, fresh_factor(), turn_banks[1])
        y1 = make_y1([z10, z11], work[4], y_banks)
        for c in (2, 3):
            for b in range(2):
                make_h1(c, b)
        put_y1(1, 0, y1, f10)
        put_y1(0, 1, y0, f01)
        put_y1(1, 1, y1, f11)
        v2_codes = gather(tab2_sb, offs2_sb, U32, "v2_codes")
        v2_scales = gather(tab2_scales_sb, offs2_sb, U8, "v2_scales")
        w2_q = [quantize_held(interleave("scalar", w2_raw[0], True, "w2_g", shared_g), "w2_0")]
        w2_q.append(quantize_held(interleave("scalar", w2_raw[1], True, "w2_g"), "w2_1"))
        z2_f = [stage[0], stage[1]]
        z20 = z1_by_scalar(2, 0, work[0], fresh_bf(), spare[0])
        h2_sb = [make_h2(w2_q[0], v2_codes, v2_scales)]
        join(h2_sb[0], 0, z2_f[0], range(4))
        z21 = z1_by_scalar(2, 1, work[2], z2_f[1][:, 2, :].bitcast(BF16), spare[1])
        h2_sb.append(make_h2(w2_q[1], v2_codes, v2_scales))
        join(h2_sb[1], 1, z2_f[1], range(4))
        y2 = make_y1([z20, z21], work[0], y_banks)
        put_y1(2, 0, y2, make_factor(2, 0, h2_sb[1][:, 3, :], h_banks[0]))
        z2_g = [interleave("scalar", z2_f[0], False, "z2_g", work[2][:].bitcast(BF16))]
        w4_q = [quantize_held(interleave("scalar", w4_raw[a], False, "w4_g"), "w4_%d" % a) for a in range(2)]
        last_stage = stage[3][:].rearrange("p j c -> p (j c)")
        z2_g.append(interleave("scalar", z2_f[1], False, "z2_g", last_stage[:, 0 : 2 * PASS].bitcast(BF16)))
        z2_q = [quantize_held(z2_g[b], "z2_%d" % b) for b in range(2)]
        put_y1(2, 1, y2, make_factor(2, 1, last_stage[:, 0 : 2 * CHUNK], h_banks[1]))

        def put_y2(nt, y2_sb):
            m_cols = slice(nt * P, (nt + 1) * P)
            bank = h_banks[(nt + 2) % 4][:].rearrange("p e n -> p (e n)")
            for a in range(2):
                nc.tensor.matmul_mx(
                    out=bank,
                    lhsT=w4_q[a][0][:, m_cols].bitcast(FP8X4),
                    lhsT_scale=w4_q[a][1][:, m_cols],
                    rhs=z2_q[a][0][:].bitcast(FP8X4),
                    rhs_scale=z2_q[a][1][:],
                    start=(a == 0),
                    stop=(a == 1),
                )
            nc.scalar.copy(y2_sb[:], bank)
            nc.vector.tensor_tensor(pages[nt][:].indirect(offs4_sb[:]), y2_sb[:], wg2_sb[:], MULT)

        put_y2(0, spare[0])
        put_y2(1, spare[1])
        z30 = z1_by_scalar(3, 0, stage[1][:].rearrange("p j c -> p (j c)"), fresh_bf(), spare[2])
        z31 = z1_by_scalar(3, 1, stage[1][:].rearrange("p j c -> p (j c)")[:, 4 * CHUNK :], fresh_bf(), spare[3])
        put_y2(2, spare[3])
        y3 = make_y1([z30, z31], work[1], turn_banks)
        put_y1(3, 0, y3, make_factor(3, 0, fresh_factor(), y_banks[0]))
        put_y1(3, 1, y3, make_factor(3, 1, fresh_factor(), y_banks[1]))
        put_y2(3, spare[2])
        for nt in range(N // P):
            nc.sync.dma_start(out[nt * P : (nt + 1) * P, :], pages[nt][:])
